import numpy as np
import ml_dtypes


def mxq(x, axis, fmt="e4m3"):
    dtype, down = {"e4m3": (ml_dtypes.float8_e4m3fn, 7), "e5m2": (ml_dtypes.float8_e5m2, 14)}[fmt]
    v = np.moveaxis(np.asarray(x, np.float32).astype(ml_dtypes.bfloat16).astype(np.float64), axis, -1)
    blocks = v.reshape(v.shape[:-1] + (-1, 32))
    amax = np.abs(blocks).max(-1, keepdims=True)
    byte = np.maximum(np.where(amax > 0, np.frexp(amax)[1] - 1 + 127, 0) - down, 1)
    scale = np.exp2(byte - 127.0)
    codes = (blocks / scale).astype(np.float32).astype(dtype).astype(np.float64)
    return np.moveaxis((codes * scale).reshape(v.shape), -1, axis)


WIDE = False


def mx_kscale(k):
    if not WIDE:
        return np.ones(k)
    levels = np.array([10, -10, 5, -5, 0])
    if k % 512:
        return np.exp2(np.random.permutation(np.resize(levels, k // 32))).repeat(32)
    a = np.empty((k // 512, 16))
    for p in range(k // 512):
        a[p, :8] = np.random.permutation(np.resize(levels, 8))
        for g in range(8):
            far = levels[np.abs(levels - a[p, g]) >= 10]
            a[p, g + 8] = far[np.random.randint(len(far))]
    return np.exp2(a.ravel()).repeat(32)


def f64(x):
    return np.asarray(x).astype(np.float64)


def striped(idx):
    return np.tile(idx.reshape(-1, 16).T, (8, 1)).astype(np.uint16)


def unstriped(offs):
    return offs[:16].T.reshape(-1).astype(np.int64)


def pack_weight(w):
    k, n = w.shape
    w = f64(np.asarray(w, np.float32).astype(ml_dtypes.bfloat16)).reshape(k // 32, 32, n)
    amax = np.abs(w).max(1)
    byte = np.clip(np.where(amax > 0, np.frexp(amax)[1] - 1 + 127 - 7, 1), 1, 254)
    scaled = (w * np.exp2(127.0 - byte)[:, None, :]).reshape(k, n).astype(np.float32)
    words = np.ascontiguousarray(scaled.reshape(k // 512, 128, 4, n).transpose(0, 1, 3, 2)).astype(ml_dtypes.float8_e4m3fn).view(np.uint8)
    return words, np.ascontiguousarray(byte.astype(np.uint8).reshape(k // 512, 16, n))


def unpack_weight(words, scales):
    g, p, n, _ = words.shape
    vals = np.ascontiguousarray(words).view(ml_dtypes.float8_e4m3fn).astype(np.float64) * np.repeat(np.exp2(scales.astype(np.float64) - 127.0), 8, axis=1)[..., None]
    return vals.transpose(0, 1, 3, 2).reshape(g * 512, n)


def relu(v):
    return np.maximum(v, 0.0)


K, T, D, S, V, N = 1024, 1024, 4, 512, 128, 256


def setup_inputs():
    n = np.random.standard_normal
    s = mx_kscale(K)[:, None]
    words, scales = pack_weight(n((K, N)) / np.sqrt(K) / s)
    return {
        "xT": (n((K, T)) * s).astype(np.float32),
        "w_words": words,
        "w_scales": scales,
        "b": (0.3 * n((N, 1))).astype(np.float32),
        "offs": striped(np.random.permutation(T)[:S]),
    }


def reference(xT, w_words, w_scales, b, offs):
    w = unpack_weight(w_words, w_scales)
    idx = unstriped(offs)
    xq = mxq(f64(xT)[:, idx], 0, "e4m3")
    y = w.T @ xq
    y = relu(y + f64(b))
    return y.reshape(N, V, D).max(axis=2)

@@ -1,0 +1,128 @@
+from contextlib import ExitStack
+
+import concourse.mybir as mybir
+
+K, T, S, V, D, N = 1024, 1024, 512, 128, 4, 256
+P = 128
+PACK = 4
+PASSES = K // (P * PACK)
+HALF = S // 2
+VH = V // 2
+FLOPS = 2 * K * S * N
+
+F32 = mybir.dt.float32
+BF16 = mybir.dt.bfloat16
+U32 = mybir.dt.uint32
+I32 = mybir.dt.int32
+U16 = mybir.dt.uint16
+U8 = mybir.dt.uint8
+FP8X4 = mybir.dt.float8_e4m3fn_x4
+COPY = mybir.ActivationFunctionType.Copy
+RELU = mybir.ActivationFunctionType.Relu
+
+
+def tile_picked_pool_lin_relu_sub_e_kernel(tc, xT, w_words, w_scales, b, offs, out):
+    nc = tc.nc
+    with ExitStack() as ctx:
+        keep = ctx.enter_context(tc.tile_pool(name="keep", bufs=1))
+        psum = ctx.enter_context(tc.psum_pool(name="psum", bufs=1))
+
+        lists = keep.tile([P, S // 16], U16, name="lists")
+        nc.sync.dma_start(lists[:], offs)
+
+        planes = xT.rearrange("(a p t) w -> a t p w", a=PASSES, t=PACK)
+        x = {}
+        for a in range(PASSES):
+            for t in range(PACK):
+                x[a, t] = keep.tile([P, T], F32, align_bytes=64, name="x%d%d" % (a, t), tag="x%d%d" % (a, t))
+        wsc = keep.tile([P, N], U8, align_bytes=64, name="wsc")
+        nc.gpsimd.memset(wsc[:].bitcast(I32), 0)
+        words = keep.tile([P, PASSES, N * 4], U8, align_bytes=64, name="words")
+        bias = [keep.tile([P, 1], F32, name="bias%d" % m) for m in range(2)]
+        for t in range(PACK):
+            nc.sync.dma_start(x[0, t][:], planes[0, t])
+        for t in range(PACK):
+            nc.sync.dma_start(x[1, t][:], planes[1, t])
+        nc.sync.dma_start(words[:, 0, :], w_words[0].rearrange("p n r -> p (n r)"))
+        for q in range(4):
+            nc.sync.dma_start(wsc[32 * q : 32 * q + 8, :].bitcast(I32), w_scales[:, 4 * q : 4 * q + 4, :].bitcast(I32))
+        nc.sync.dma_start(words[:, 1, :], w_words[1].rearrange("p n r -> p (n r)"))
+        for m in range(2):
+            nc.sync.dma_start(bias[m][:], b[m * P : (m + 1) * P, :])
+
+        warm = keep.tile([P, 1], F32, name="warm")
+        nc.vector.memset(warm[:], 0.0)
+        nc.scalar.activation(warm[:], warm[:], RELU)
+
+        codes = {1: keep.tile([P, S], U32, align_bytes=64, name="codes1")}
+        scales = [keep.tile([P, S], U8, align_bytes=64, name="scales%d" % a) for a in range(PASSES)]
+        grouped0 = keep.tile([P, S, PACK], BF16, align_bytes=64, name="grouped0")
+        grouped1 = keep.tile([P, S, PACK], BF16, align_bytes=64, name="grouped1")
+        xb = [keep.tile([P, T], BF16, align_bytes=64, name="xb%d" % t) for t in range(2)]
+        g = [keep.tile([P, PACK, S], F32, name="g%d" % a) for a in range(PASSES)]
+        acc = {}
+        for h in range(2):
+            for m in range(2):
+                acc[m, h] = psum.tile([P, HALF], F32, name="acc%d%d" % (m, h))
+
+        def gather(a, t, h=None):
+            if h is None:
+                nc.vector.tensor_copy(g[a][:, t, :], x[a, t][:].indirect(lists[:]))
+            else:
+                nc.vector.tensor_copy(g[a][:, t, h * HALF : (h + 1) * HALF], x[a, t][:].indirect(lists[:, h * 16 : (h + 1) * 16]))
+
+        def quantize(a, lo, hi, src):
+            nc.vector.quantize_mx(
+                out=codes[a][:, lo:hi].bitcast(FP8X4),
+                scales=scales[a][:, lo:hi],
+                in_=src[:, lo:hi, :].rearrange("p n t -> p (n t)"),
+            )
+
+        def product(a, m, h):
+            cols = slice(h * HALF, (h + 1) * HALF)
+            nc.tensor.matmul_mx(
+                out=acc[m, h][:],
+                lhsT=words[:, a, m * P * 4 : (m + 1) * P * 4].bitcast(FP8X4),
+                lhsT_scale=wsc[4 * a :, m * P : (m + 1) * P],
+                rhs=codes[a][:, cols].bitcast(FP8X4),
+                rhs_scale=scales[a][:, cols],
+                start=(a == 0),
+                stop=(a == PASSES - 1),
+            )
+
+        for t in range(PACK):
+            gather(0, t)
+            if t == 1:
+                nc.scalar.copy(grouped0[:, :, 0:2], g[0][:, 0:2, :].rearrange("p t n -> p n t"))
+        nc.scalar.copy(grouped0[:, 0:HALF, 2:4], g[0][:, 2:4, 0:HALF].rearrange("p t n -> p n t"))
+        nc.vector.tensor_copy(grouped0[:, HALF:S, 2:4], g[0][:, 2:4, HALF:S].rearrange("p t n -> p n t"))
+        for t in range(2):
+            nc.vector.tensor_copy(xb[t][:], x[1, t][:])
+            nc.scalar.activation(grouped1[:, :, t], xb[t][:].indirect(lists[:]), COPY)
+        gather(1, 2)
+        codes[0] = keep.tile([P, S], U32, align_bytes=64, name="codes0", tag="x12")
+        quantize(0, 0, S, grouped0)
+        for h in range(2):
+            for m in range(2):
+                product(0, m, h)
+        gather(1, 3, 0)
+        gather(1, 3, 1)
+        nc.scalar.copy(grouped1[:, 0:HALF, 2:4], g[1][:, 2:4, 0:HALF].rearrange("p t n -> p n t"))
+        nc.vector.tensor_copy(grouped1[:, HALF:S, 2:4], g[1][:, 2:4, HALF:S].rearrange("p t n -> p n t"))
+        result = [keep.tile([P, 2, VH], F32, name="result%d" % h) for h in range(2)]
+        best = [keep.tile([P, 2, VH], F32, name="best%d" % h) for h in range(2)]
+        out_v = out.rearrange("(m p) v -> p m v", p=P)
+        for h in (1, 0):
+            quantize(1, h * HALF, (h + 1) * HALF, grouped1)
+            for m in range(2):
+                product(1, m, h)
+        for h in (1, 0):
+            for m in range(2):
+                nc.vector.tensor_reduce(
+                    best[h][:, m, :],
+                    acc[m, h][:].rearrange("p (v d) -> p v d", d=D),
+                    axis=mybir.AxisListType.X,
+                    op=mybir.AluOpType.max,
+                )
+                nc.scalar.activation(result[h][:, m, :], best[h][:, m, :], RELU, bias=bias[m][:])
+            nc.scalar.dma_start(out_v[:, :, h * VH : (h + 1) * VH], result[h][:])

@@ -18,7 +18,6 @@ U16 = mybir.dt.uint16
 U8 = mybir.dt.uint8
 FP8X4 = mybir.dt.float8_e4m3fn_x4
 COPY = mybir.ActivationFunctionType.Copy
-RELU = mybir.ActivationFunctionType.Relu
 
 
 def tile_picked_pool_lin_relu_sub_e_kernel(tc, xT, w_words, w_scales, b, offs, out):
@@ -49,10 +48,6 @@ def tile_picked_pool_lin_relu_sub_e_kernel(tc, xT, w_words, w_scales, b, offs, o
         nc.sync.dma_start(words[:, 1, :], w_words[1].rearrange("p n r -> p (n r)"))
         for m in range(2):
             nc.sync.dma_start(bias[m][:], b[m * P : (m + 1) * P, :])
-
-        warm = keep.tile([P, 1], F32, name="warm")
-        nc.vector.memset(warm[:], 0.0)
-        nc.scalar.activation(warm[:], warm[:], RELU)
 
         codes = {1: keep.tile([P, S], U32, align_bytes=64, name="codes1")}
         scales = [keep.tile([P, S], U8, align_bytes=64, name="scales%d" % a) for a in range(PASSES)]
@@ -99,16 +94,17 @@ def tile_picked_pool_lin_relu_sub_e_kernel(tc, xT, w_words, w_scales, b, offs, o
         for t in range(2):
             nc.vector.tensor_copy(xb[t][:], x[1, t][:])
             nc.scalar.activation(grouped1[:, :, t], xb[t][:].indirect(lists[:]), COPY)
-        gather(1, 2)
-        codes[0] = keep.tile([P, S], U32, align_bytes=64, name="codes0", tag="x12")
+        codes[0] = keep.tile([P, S], U32, align_bytes=64, name="codes0", tag="x11")
         quantize(0, 0, S, grouped0)
-        for h in range(2):
+        for h in (1, 0):
             for m in range(2):
                 product(0, m, h)
-        gather(1, 3, 0)
+        gather(1, 2)
         gather(1, 3, 1)
-        nc.scalar.copy(grouped1[:, 0:HALF, 2:4], g[1][:, 2:4, 0:HALF].rearrange("p t n -> p n t"))
-        nc.vector.tensor_copy(grouped1[:, HALF:S, 2:4], g[1][:, 2:4, HALF:S].rearrange("p t n -> p n t"))
+        gather(1, 3, 0)
+        for h in (1, 0):
+            cols = slice(h * HALF, (h + 1) * HALF)
+            nc.vector.tensor_copy(grouped1[:, cols, 2:4], g[1][:, 2:4, cols].rearrange("p t n -> p n t"))
         result = [keep.tile([P, 2, VH], F32, name="result%d" % h) for h in range(2)]
         best = [keep.tile([P, 2, VH], F32, name="best%d" % h) for h in range(2)]
         out_v = out.rearrange("(m p) v -> p m v", p=P)
@@ -124,5 +120,13 @@ def tile_picked_pool_lin_relu_sub_e_kernel(tc, xT, w_words, w_scales, b, offs, o
                     axis=mybir.AxisListType.X,
                     op=mybir.AluOpType.max,
                 )
-                nc.scalar.activation(result[h][:, m, :], best[h][:, m, :], RELU, bias=bias[m][:])
-            nc.scalar.dma_start(out_v[:, :, h * VH : (h + 1) * VH], result[h][:])
+            for m in range(2):
+                nc.vector.tensor_scalar(
+                    result[h][:, m, :],
+                    best[h][:, m, :],
+                    scalar1=bias[m][:],
+                    scalar2=0.0,
+                    op0=mybir.AluOpType.add,
+                    op1=mybir.AluOpType.max,
+                )
+            nc.sync.dma_start(out_v[:, :, h * VH : (h + 1) * VH], result[h][:])

@@ -40,76 +40,81 @@ def tile_picked_pool_lin_relu_sub_e_kernel(tc, xT, w_words, w_scales, b, offs, o
         bias = [keep.tile([P, 1], F32, name="bias%d" % m) for m in range(2)]
         for t in range(PACK):
             nc.sync.dma_start(x[0, t][:], planes[0, t])
+            if t == 0:
+                for q in range(4):
+                    nc.sync.dma_start(wsc[32 * q : 32 * q + 8, :].bitcast(I32), w_scales[:, 4 * q : 4 * q + 4, :].bitcast(I32))
         for t in range(PACK):
             nc.sync.dma_start(x[1, t][:], planes[1, t])
         nc.sync.dma_start(words[:, 0, :], w_words[0].rearrange("p n r -> p (n r)"))
-        for q in range(4):
-            nc.sync.dma_start(wsc[32 * q : 32 * q + 8, :].bitcast(I32), w_scales[:, 4 * q : 4 * q + 4, :].bitcast(I32))
         nc.sync.dma_start(words[:, 1, :], w_words[1].rearrange("p n r -> p (n r)"))
         for m in range(2):
             nc.sync.dma_start(bias[m][:], b[m * P : (m + 1) * P, :])
 
         codes = {1: keep.tile([P, S], U32, align_bytes=64, name="codes1")}
         scales = [keep.tile([P, S], U8, align_bytes=64, name="scales%d" % a) for a in range(PASSES)]
-        grouped0 = keep.tile([P, S, PACK], BF16, align_bytes=64, name="grouped0")
-        grouped1 = keep.tile([P, S, PACK], BF16, align_bytes=64, name="grouped1")
+        grouped = [keep.tile([P, S, PACK], BF16, align_bytes=64, name="grouped%d" % a) for a in range(PASSES)]
+        paired = [keep.tile([P, 2, S, 2], BF16, align_bytes=64, name="paired%d" % a) for a in range(PASSES)]
         xb = [keep.tile([P, T], BF16, align_bytes=64, name="xb%d" % t) for t in range(2)]
-        g = [keep.tile([P, PACK, S], F32, name="g%d" % a) for a in range(PASSES)]
         acc = {}
         for h in range(2):
             for m in range(2):
                 acc[m, h] = psum.tile([P, HALF], F32, name="acc%d%d" % (m, h))
 
-        def gather(a, t, h=None):
-            if h is None:
-                nc.vector.tensor_copy(g[a][:, t, :], x[a, t][:].indirect(lists[:]))
-            else:
-                nc.vector.tensor_copy(g[a][:, t, h * HALF : (h + 1) * HALF], x[a, t][:].indirect(lists[:, h * 16 : (h + 1) * 16]))
+        def half(h):
+            return slice(h * HALF, (h + 1) * HALF)
 
-        def quantize(a, lo, hi, src):
+        def gather(a, t, h=None):
+            cols = slice(0, S) if h is None else half(h)
+            nc.vector.tensor_copy(
+                paired[a][:, t // 2, cols, t % 2],
+                x[a, t][:].indirect(lists[:, cols.start // 16 : cols.stop // 16]),
+            )
+
+        def merge(copy, a, h):
+            dst = grouped[a][:].rearrange("p n t -> p (n t)").bitcast(F32).rearrange("p (n u) -> p n u", u=2)
+            src = paired[a][:].rearrange("p u n e -> p (u n e)").bitcast(F32).rearrange("p (u n) -> p n u", u=2)
+            copy(dst[:, half(h), :], src[:, half(h), :])
+
+        def quantize(a, lo, hi):
             nc.vector.quantize_mx(
                 out=codes[a][:, lo:hi].bitcast(FP8X4),
                 scales=scales[a][:, lo:hi],
-                in_=src[:, lo:hi, :].rearrange("p n t -> p (n t)"),
+                in_=grouped[a][:, lo:hi, :].rearrange("p n t -> p (n t)"),
             )
 
         def product(a, m, h):
-            cols = slice(h * HALF, (h + 1) * HALF)
             nc.tensor.matmul_mx(
                 out=acc[m, h][:],
                 lhsT=words[:, a, m * P * 4 : (m + 1) * P * 4].bitcast(FP8X4),
                 lhsT_scale=wsc[4 * a :, m * P : (m + 1) * P],
-                rhs=codes[a][:, cols].bitcast(FP8X4),
-                rhs_scale=scales[a][:, cols],
+                rhs=codes[a][:, half(h)].bitcast(FP8X4),
+                rhs_scale=scales[a][:, half(h)],
                 start=(a == 0),
                 stop=(a == PASSES - 1),
             )
 
         for t in range(PACK):
             gather(0, t)
-            if t == 1:
-                nc.scalar.copy(grouped0[:, :, 0:2], g[0][:, 0:2, :].rearrange("p t n -> p n t"))
-        nc.scalar.copy(grouped0[:, 0:HALF, 2:4], g[0][:, 2:4, 0:HALF].rearrange("p t n -> p n t"))
-        nc.vector.tensor_copy(grouped0[:, HALF:S, 2:4], g[0][:, 2:4, HALF:S].rearrange("p t n -> p n t"))
+        merge(nc.scalar.copy, 0, 0)
+        merge(nc.vector.tensor_copy, 0, 1)
         for t in range(2):
             nc.vector.tensor_copy(xb[t][:], x[1, t][:])
-            nc.scalar.activation(grouped1[:, :, t], xb[t][:].indirect(lists[:]), COPY)
+            nc.scalar.activation(paired[1][:, 0, :, t], xb[t][:].indirect(lists[:]), COPY)
         codes[0] = keep.tile([P, S], U32, align_bytes=64, name="codes0", tag="x11")
-        quantize(0, 0, S, grouped0)
+        quantize(0, 0, S)
         for h in (1, 0):
             for m in range(2):
                 product(0, m, h)
         gather(1, 2)
         gather(1, 3, 1)
         gather(1, 3, 0)
-        for h in (1, 0):
-            cols = slice(h * HALF, (h + 1) * HALF)
-            nc.vector.tensor_copy(grouped1[:, cols, 2:4], g[1][:, 2:4, cols].rearrange("p t n -> p n t"))
+        merge(nc.vector.tensor_copy, 1, 1)
+        merge(nc.vector.tensor_copy, 1, 0)
         result = [keep.tile([P, 2, VH], F32, name="result%d" % h) for h in range(2)]
         best = [keep.tile([P, 2, VH], F32, name="best%d" % h) for h in range(2)]
         out_v = out.rearrange("(m p) v -> p m v", p=P)
         for h in (1, 0):
-            quantize(1, h * HALF, (h + 1) * HALF, grouped1)
+            quantize(1, h * HALF, (h + 1) * HALF)
             for m in range(2):
                 product(1, m, h)
         for h in (1, 0):

@@ -6,8 +6,7 @@ K, T, S, V, D, N = 1024, 1024, 512, 128, 4, 256
 P = 128
 PACK = 4
 PASSES = K // (P * PACK)
-HALF = S // 2
-VH = V // 2
+PIECES = ((0, 256), (256, 384), (384, 512))
 FLOPS = 2 * K * S * N
 
 F32 = mybir.dt.float32
@@ -56,82 +55,85 @@ def tile_picked_pool_lin_relu_sub_e_kernel(tc, xT, w_words, w_scales, b, offs, o
         paired = [keep.tile([P, 2, S, 2], BF16, align_bytes=64, name="paired%d" % a) for a in range(PASSES)]
         xb = [keep.tile([P, T], BF16, align_bytes=64, name="xb%d" % t) for t in range(2)]
         acc = {}
-        for h in range(2):
+        for i, (lo, hi) in enumerate(PIECES):
             for m in range(2):
-                acc[m, h] = psum.tile([P, HALF], F32, name="acc%d%d" % (m, h))
+                acc[m, i] = psum.tile([P, hi - lo], F32, name="acc%d%d" % (m, i))
 
-        def half(h):
-            return slice(h * HALF, (h + 1) * HALF)
-
-        def gather(a, t, h=None):
-            cols = slice(0, S) if h is None else half(h)
+        def gather(a, t, lo=0, hi=S):
             nc.vector.tensor_copy(
-                paired[a][:, t // 2, cols, t % 2],
-                x[a, t][:].indirect(lists[:, cols.start // 16 : cols.stop // 16]),
+                paired[a][:, t // 2, lo:hi, t % 2],
+                x[a, t][:].indirect(lists[:, lo // 16 : hi // 16]),
             )
 
-        def merge(copy, a, h):
+        def merge(copy, a, lo=0, hi=S):
             dst = grouped[a][:].rearrange("p n t -> p (n t)").bitcast(F32).rearrange("p (n u) -> p n u", u=2)
             src = paired[a][:].rearrange("p u n e -> p (u n e)").bitcast(F32).rearrange("p (u n) -> p n u", u=2)
-            copy(dst[:, half(h), :], src[:, half(h), :])
+            copy(dst[:, lo:hi, :], src[:, lo:hi, :])
 
-        def quantize(a, lo, hi):
+        def quantize(a, lo=0, hi=S):
             nc.vector.quantize_mx(
                 out=codes[a][:, lo:hi].bitcast(FP8X4),
                 scales=scales[a][:, lo:hi],
                 in_=grouped[a][:, lo:hi, :].rearrange("p n t -> p (n t)"),
             )
 
-        def product(a, m, h):
+        def product(a, m, i):
+            cols = slice(*PIECES[i])
             nc.tensor.matmul_mx(
-                out=acc[m, h][:],
+                out=acc[m, i][:],
                 lhsT=words[:, a, m * P * 4 : (m + 1) * P * 4].bitcast(FP8X4),
                 lhsT_scale=wsc[4 * a :, m * P : (m + 1) * P],
-                rhs=codes[a][:, half(h)].bitcast(FP8X4),
-                rhs_scale=scales[a][:, half(h)],
+                rhs=codes[a][:, cols].bitcast(FP8X4),
+                rhs_scale=scales[a][:, cols],
                 start=(a == 0),
                 stop=(a == PASSES - 1),
             )
 
         for t in range(PACK):
             gather(0, t)
-        merge(nc.scalar.copy, 0, 0)
-        merge(nc.vector.tensor_copy, 0, 1)
+        merge(nc.scalar.copy, 0)
         for t in range(2):
             nc.vector.tensor_copy(xb[t][:], x[1, t][:])
             nc.scalar.activation(paired[1][:, 0, :, t], xb[t][:].indirect(lists[:]), COPY)
         codes[0] = keep.tile([P, S], U32, align_bytes=64, name="codes0", tag="x11")
-        quantize(0, 0, S)
-        for h in (1, 0):
+        quantize(0)
+        for i in range(3):
             for m in range(2):
-                product(0, m, h)
+                product(0, m, i)
         gather(1, 2)
-        gather(1, 3, 1)
-        gather(1, 3, 0)
-        merge(nc.vector.tensor_copy, 1, 1)
-        merge(nc.vector.tensor_copy, 1, 0)
-        result = [keep.tile([P, 2, VH], F32, name="result%d" % h) for h in range(2)]
-        best = [keep.tile([P, 2, VH], F32, name="best%d" % h) for h in range(2)]
-        out_v = out.rearrange("(m p) v -> p m v", p=P)
-        for h in (1, 0):
-            quantize(1, h * HALF, (h + 1) * HALF)
+        gather(1, 3, *PIECES[0])
+        gather(1, 3, *PIECES[1])
+        merge(nc.vector.tensor_copy, 1, *PIECES[0])
+        gather(1, 3, *PIECES[2])
+        quantize(1, *PIECES[0])
+        merge(nc.vector.tensor_copy, 1, *PIECES[1])
+        merge(nc.vector.tensor_copy, 1, *PIECES[2])
+        quantize(1, *PIECES[1])
+        quantize(1, *PIECES[2])
+        for i in range(3):
             for m in range(2):
-                product(1, m, h)
-        for h in (1, 0):
+                product(1, m, i)
+        best = [keep.tile([P, 2, V // 2], F32, name="best%d" % h) for h in range(2)]
+        result = {(h, m): keep.tile([P, V // 2], F32, name="result%d%d" % (h, m)) for h in range(2) for m in range(2)}
+        for i, (lo, hi) in enumerate(PIECES):
+            h = lo * 2 // S
+            v0 = lo // D - h * V // 2
             for m in range(2):
                 nc.vector.tensor_reduce(
-                    best[h][:, m, :],
-                    acc[m, h][:].rearrange("p (v d) -> p v d", d=D),
+                    best[h][:, m, v0 : v0 + (hi - lo) // D],
+                    acc[m, i][:].rearrange("p (v d) -> p v d", d=D),
                     axis=mybir.AxisListType.X,
                     op=mybir.AluOpType.max,
                 )
+            if i == 1:
+                continue
             for m in range(2):
                 nc.vector.tensor_scalar(
-                    result[h][:, m, :],
+                    result[h, m][:],
                     best[h][:, m, :],
                     scalar1=bias[m][:],
                     scalar2=0.0,
                     op0=mybir.AluOpType.add,
                     op1=mybir.AluOpType.max,
                 )
-            nc.sync.dma_start(out_v[:, :, h * VH : (h + 1) * VH], result[h][:])
+                nc.sync.dma_start(out[m * P : (m + 1) * P, h * V // 2 : (h + 1) * V // 2], result[h, m][:])

from contextlib import ExitStack

import concourse.mybir as mybir

K, T, S, V, D, N = 1024, 1024, 512, 128, 4, 256
P = 128
PACK = 4
PASSES = K // (P * PACK)
PIECES = ((0, 256), (256, 384), (384, 512))
FLOPS = 2 * K * S * N

F32 = mybir.dt.float32
BF16 = mybir.dt.bfloat16
U32 = mybir.dt.uint32
I32 = mybir.dt.int32
U16 = mybir.dt.uint16
U8 = mybir.dt.uint8
FP8X4 = mybir.dt.float8_e4m3fn_x4
COPY = mybir.ActivationFunctionType.Copy


def tile_picked_pool_lin_relu_sub_e_kernel(tc, xT, w_words, w_scales, b, offs, out):
    nc = tc.nc
    with ExitStack() as ctx:
        keep = ctx.enter_context(tc.tile_pool(name="keep", bufs=1))
        psum = ctx.enter_context(tc.psum_pool(name="psum", bufs=1))

        lists = keep.tile([P, S // 16], U16, name="lists")
        nc.sync.dma_start(lists[:], offs)

        planes = xT.rearrange("(a p t) w -> a t p w", a=PASSES, t=PACK)
        x = {}
        for a in range(PASSES):
            for t in range(PACK):
                x[a, t] = keep.tile([P, T], F32, align_bytes=64, name="x%d%d" % (a, t), tag="x%d%d" % (a, t))
        wsc = keep.tile([P, N], U8, align_bytes=64, name="wsc")
        nc.gpsimd.memset(wsc[:].bitcast(I32), 0)
        words = keep.tile([P, PASSES, N * 4], U8, align_bytes=64, name="words")
        bias = [keep.tile([P, 1], F32, name="bias%d" % m) for m in range(2)]
        for t in range(PACK):
            nc.sync.dma_start(x[0, t][:], planes[0, t])
            if t == 0:
                for q in range(4):
                    nc.sync.dma_start(wsc[32 * q : 32 * q + 8, :].bitcast(I32), w_scales[:, 4 * q : 4 * q + 4, :].bitcast(I32))
        for t in range(PACK):
            nc.sync.dma_start(x[1, t][:], planes[1, t])
        nc.sync.dma_start(words[:, 0, :], w_words[0].rearrange("p n r -> p (n r)"))
        nc.sync.dma_start(words[:, 1, :], w_words[1].rearrange("p n r -> p (n r)"))
        for m in range(2):
            nc.sync.dma_start(bias[m][:], b[m * P : (m + 1) * P, :])

        codes = {1: keep.tile([P, S], U32, align_bytes=64, name="codes1")}
        scales = [keep.tile([P, S], U8, align_bytes=64, name="scales%d" % a) for a in range(PASSES)]
        grouped = [keep.tile([P, S, PACK], BF16, align_bytes=64, name="grouped%d" % a) for a in range(PASSES)]
        paired = [keep.tile([P, 2, S, 2], BF16, align_bytes=64, name="paired%d" % a) for a in range(PASSES)]
        xb = [keep.tile([P, T], BF16, align_bytes=64, name="xb%d" % t) for t in range(2)]
        acc = {}
        for i, (lo, hi) in enumerate(PIECES):
            for m in range(2):
                acc[m, i] = psum.tile([P, hi - lo], F32, name="acc%d%d" % (m, i))

        def gather(a, t, lo=0, hi=S):
            nc.vector.tensor_copy(
                paired[a][:, t // 2, lo:hi, t % 2],
                x[a, t][:].indirect(lists[:, lo // 16 : hi // 16]),
            )

        def merge(copy, a, lo=0, hi=S):
            dst = grouped[a][:].rearrange("p n t -> p (n t)").bitcast(F32).rearrange("p (n u) -> p n u", u=2)
            src = paired[a][:].rearrange("p u n e -> p (u n e)").bitcast(F32).rearrange("p (u n) -> p n u", u=2)
            copy(dst[:, lo:hi, :], src[:, lo:hi, :])

        def quantize(a, lo=0, hi=S):
            nc.vector.quantize_mx(
                out=codes[a][:, lo:hi].bitcast(FP8X4),
                scales=scales[a][:, lo:hi],
                in_=grouped[a][:, lo:hi, :].rearrange("p n t -> p (n t)"),
            )

        def product(a, m, i):
            cols = slice(*PIECES[i])
            nc.tensor.matmul_mx(
                out=acc[m, i][:],
                lhsT=words[:, a, m * P * 4 : (m + 1) * P * 4].bitcast(FP8X4),
                lhsT_scale=wsc[4 * a :, m * P : (m + 1) * P],
                rhs=codes[a][:, cols].bitcast(FP8X4),
                rhs_scale=scales[a][:, cols],
                start=(a == 0),
                stop=(a == PASSES - 1),
            )

        for t in range(PACK):
            gather(0, t)
        merge(nc.scalar.copy, 0)
        for t in range(2):
            nc.vector.tensor_copy(xb[t][:], x[1, t][:])
            nc.scalar.activation(paired[1][:, 0, :, t], xb[t][:].indirect(lists[:]), COPY)
        codes[0] = keep.tile([P, S], U32, align_bytes=64, name="codes0", tag="x11")
        quantize(0)
        for i in range(3):
            for m in range(2):
                product(0, m, i)
        gather(1, 2)
        gather(1, 3, *PIECES[0])
        gather(1, 3, *PIECES[1])
        merge(nc.vector.tensor_copy, 1, *PIECES[0])
        gather(1, 3, *PIECES[2])
        quantize(1, *PIECES[0])
        merge(nc.vector.tensor_copy, 1, *PIECES[1])
        merge(nc.vector.tensor_copy, 1, *PIECES[2])
        quantize(1, *PIECES[1])
        quantize(1, *PIECES[2])
        for i in range(3):
            for m in range(2):
                product(1, m, i)
        best = [keep.tile([P, 2, V // 2], F32, name="best%d" % h) for h in range(2)]
        result = {(h, m): keep.tile([P, V // 2], F32, name="result%d%d" % (h, m)) for h in range(2) for m in range(2)}
        for i, (lo, hi) in enumerate(PIECES):
            h = lo * 2 // S
            v0 = lo // D - h * V // 2
            for m in range(2):
                nc.vector.tensor_reduce(
                    best[h][:, m, v0 : v0 + (hi - lo) // D],
                    acc[m, i][:].rearrange("p (v d) -> p v d", d=D),
                    axis=mybir.AxisListType.X,
                    op=mybir.AluOpType.max,
                )
            if i == 1:
                continue
            for m in range(2):
                nc.vector.tensor_scalar(
                    result[h, m][:],
                    best[h][:, m, :],
                    scalar1=bias[m][:],
                    scalar2=0.0,
                    op0=mybir.AluOpType.add,
                    op1=mybir.AluOpType.max,
                )
                nc.sync.dma_start(out[m * P : (m + 1) * P, h * V // 2 : (h + 1) * V // 2], result[h, m][:])
